import numpy as np, ml_dtypes
CORES = [66,74,82,90,194,202,210,218]
N = 8
import mx_ref
NC, K = 128, 2
CNT = [[0,36,32,0,40,8,12,0],[24,0,12,52,8,0,12,20],[44,0,0,0,36,24,12,12],[12,0,12,0,32,36,32,4],[4,20,4,32,0,24,0,44],[24,4,8,20,0,0,36,36],[12,36,24,24,0,20,0,12],[8,32,36,0,12,16,24,0]]
OFF = [[sum(c[:e]) for e in range(N + 1)] for c in CNT]
BF = ml_dtypes.bfloat16
def setup_inputs(rng):
    def f(*shape):
        return mx_ref.flush((rng.standard_normal(shape, dtype=np.float32) * np.exp2(rng.integers(-2, 3, shape[:-1] + (1,)))).astype(BF))
    return {"x": f(N, 128, 4 * NC), "w": f(N, 128, 512)}
def setup_inputs_blocks(rng):
    d = setup_inputs(rng)
    for k in ("x", "w"): d[k] = mx_ref.spread(d[k], rng, 4)
    return d
def setup_inputs_wide(rng):
    d = setup_inputs(rng)
    for k in ("x", "w"): d[k] = mx_ref.flush((d[k].astype(np.float32) * np.exp2(rng.integers(-8, 9, (N, 1, 1))).astype(np.float32)).astype(BF))
    return d
def setup_inputs_zeros(rng):
    d = setup_inputs(rng); v = d["x"].reshape(N, 128, -1, 4).copy()
    v[np.broadcast_to((rng.random((N, 1, v.shape[2], 1)) < 0.33), v.shape)] = 0
    d["x"] = v.reshape(d["x"].shape)
    return d
def reference(x, w):
    y = np.zeros((N, 128, K * NC), np.float32)
    for e in range(N):
        t = np.concatenate([x[j][:, 4 * OFF[j][(e - k) % N]:4 * OFF[j][(e - k) % N + 1]] for k in range(K) for j in range(N)], axis=1)
        y[e] = mx_ref.matmul(mx_ref.quantize(w[e]), mx_ref.quantize(t))
    return {"y": y}

@@ -1,0 +1,227 @@
+from concourse.bass import DstId, RemoteDMATransfer
+from concourse.mybir import dt, ActivationFunctionType
+
+NC = 128
+ALIGN = 16
+SCRATCH = {
+    "xb": ("sbuf", [128, 8 * NC], "bfloat16"),
+    "wb": ("sbuf", [128, 4 * NC], "bfloat16"),
+    "wq": ("sbuf", [128, NC], "float8_e4m3fn_x4"),
+    "ws": ("sbuf", [128, NC], "uint8"),
+    "q": ("sbuf", [128, 896], "float8_e4m3fn_x4"),
+    "s": ("sbuf", [128, 896], "uint8"),
+    "ps": ("psum", [128, 2048], "float32"),
+    "yt": ("sbuf", [128, 2 * NC], "float32"),
+}
+SEMAPHORES = ["lx", "le", "lw", "q1", "q2", "qw", "cx", "ar0", "ar1", "ar2", "ls", "mm0", "mm1", "mm2", "mm3", "vd", "sd", "st"]
+
+
+def cyc(start, n):
+    out = []
+    start %= NC
+    while n:
+        m = min(n, NC - start)
+        out.append((start, m))
+        start, n = (start + m) % NC, n - m
+    return out
+
+
+def make_plan(T, topo):
+    cores, cnt = T.cores, T.tables["CNT"]
+    N = len(cores)
+    off = [[sum(c[:e]) for e in range(N + 1)] for c in cnt]
+    peers = [[j for j in range(N) if topo.host(cores[j]) == topo.host(cores[r])] for r in range(N)]
+    partner = [next(j for j in range(N) if topo.host(cores[j]) != topo.host(cores[r]) and topo.chip(cores[j]) == topo.chip(cores[r]))
+               for r in range(N)]
+    blk = [[(peers[r][0] - 1 + i) % N for i in range(len(peers[r]) + 1)] for r in range(N)]
+    nb = len(blk[0])
+
+    def cross(s, L):
+        s1 = (off[s][blk[s][L]] + cnt[s][blk[s][L]]) % NC
+        c = blk[partner[s]]
+        return s1, (off[s][c[0]] - s1) % NC, sum(cnt[s][f] for f in c)
+
+    def windows(r, L, M, s, padl, wc):
+        own, rv = [cnt[r][f] for f in blk[r]], [cnt[s][f] for f in blk[r]]
+        res = {}
+        for k, d in enumerate(peers[r]):
+            if d == r:
+                continue
+            o = []
+            if L >= k + 1:
+                a = NC - sum(own[k:L + 1])
+                o.append((NC + padl + sum(rv[:k + 2]) - a, a))
+            if M <= k:
+                a = NC + padl + sum(rv[:k])
+                o.append((NC + wc + sum(own[M:k + 2]) - a, a))
+            if not o:
+                return None
+            res[d] = min(o)
+        return res
+
+    plan = [None] * N
+    for r in range(N):
+        if plan[r]:
+            continue
+        p = partner[r]
+        best = None
+        for Lr in range(nb - 1):
+            for Lp in range(nb - 1):
+                two = []
+                for me, frm, Lm, Lf in ((r, p, Lr, Lp), (p, r, Lp, Lr)):
+                    s1, at, w = cross(frm, Lf)
+                    pad = -w % ALIGN
+                    cand = []
+                    for padl in range(0, pad + 1, 4):
+                        if padl > at or at + w + pad - padl > NC:
+                            continue
+                        for M in range(nb - 1):
+                            win = windows(me, Lm, M, frm, padl, w + pad)
+                            if win:
+                                ws = [v[0] for v in win.values()]
+                                cand.append((max(ws), sum(ws), -M, padl, at - padl, w + pad, win))
+                    if cand:
+                        two.append(min(cand, key=lambda c: c[:4]))
+                if len(two) == 2:
+                    key = (max(two[0][0], two[1][0]), two[0][0] + two[1][0], two[0][1] + two[1][1], Lr + Lp)
+                    if best is None or key < best[0]:
+                        best = (key, two, (Lr, Lp))
+        for me, frm, c, L in ((r, p, best[1][0], best[2][0]), (p, r, best[1][1], best[2][1])):
+            M = -c[2]
+            plan[me] = {"from": frm, "W": c[0], "recv_at": c[4], "wc": c[5], "win": {d: v[1] for d, v in c[6].items()},
+                        "s1": cross(me, L)[0], "s2": off[me][blk[me][M]], "E": sum(cnt[me][f] for f in blk[me][M:])}
+    for r in range(N):
+        P = plan[r]
+        P["send_at"] = plan[partner[r]]["recv_at"]
+        P["send_w"] = plan[partner[r]]["wc"]
+        P["tile1"] = [(r, (P["s1"] + i) % NC) for i in range(NC)]
+    for r in range(N):
+        P = plan[r]
+        arrived = plan[P["from"]]["tile1"][P["recv_at"]:P["recv_at"] + P["wc"]]
+        extra = [(r, (P["s2"] + i) % NC) for i in range(P["E"])]
+        P["cols"] = P["tile1"] + arrived + extra + P["tile1"][:NC - P["E"]]
+        P["base"] = len(P["cols"])
+        P["order"] = sorted((j for j in peers[r] if j != r),
+                            key=lambda j: 0 if topo.mates(cores[j], cores[r]) else 1 if topo.same_plane(cores[j], cores[r]) else 2)
+    for e in range(N):
+        P = plan[e]
+        P["slot"], at, lay = {}, P["base"], list(P["cols"])
+        banks = [(0, NC + P["wc"])]
+        for r in P["order"]:
+            R = plan[r]
+            P["slot"][r] = at
+            a = R["win"][e]
+            lay += R["cols"][a:a + R["W"]]
+            at += R["W"]
+            banks.append((at - max(R["W"], NC), at))
+        P["banks"] = banks
+        want = [(j, off[j][(e - k) % N] + i) for k in range(2) for j in range(N) for i in range(cnt[j][(e - k) % N])]
+        runs = []
+        for c, lab in enumerate(want):
+            b, pos = next((b, i) for b, (lo, hi) in enumerate(banks) for i in range(lo, hi) if lay[i] == lab)
+            pos -= banks[b][0]
+            if runs and runs[-1][0] == b and runs[-1][1] + runs[-1][3] == pos:
+                runs[-1][3] += 1
+            else:
+                runs.append([b, pos, c, 1])
+        P["runs"] = runs
+    return plan
+
+
+def bits(mask):
+    return [1 << i for i in range(mask.bit_length()) if (mask >> i) & 1]
+
+
+def rank_program(g, core, T, topo):
+    rank = T.rank_of(core)
+    if rank is None:
+        return
+    plan = make_plan(T, topo)
+    P, S, cores = plan[rank], T.sem, T.cores
+    E, wc, W = P["E"], P["wc"], P["W"]
+
+    pieces, at = cyc(P["s1"], NC), E
+    for i, (a, n) in enumerate(pieces):
+        (g.sync if i == 0 else g.scalar).dma_start(T.xb[:, 4 * at:4 * (at + n)], T.x[:, 4 * a:4 * (a + n)]).then_inc(S.lx, 16)
+        at += n
+    extra, at = cyc(P["s2"], E), 0
+    for a, n in extra:
+        g.sync.dma_start(T.xb[:, 4 * at:4 * (at + n)], T.x[:, 4 * a:4 * (a + n)]).then_inc(S.le, 16)
+        at += n
+    nx, ne = 16 * len(pieces), 16 * len(extra)
+    g.scalar.wait_ge(S.lx, nx)
+    g.scalar.dma_start(T.wb[:], T.w[:]).then_inc(S.lw, 16)
+
+    v = g.vector
+    v.wait_ge(S.lx, nx)
+    v.quantize_mx(T.q[:, 0:NC], T.s[:, 0:NC], T.xb[:, 4 * E:4 * (E + NC)]).then_inc(S.q1, 1)
+    if ne:
+        v.wait_ge(S.le, ne)
+    t2 = NC + wc
+    v.quantize_mx(T.q[:, t2:t2 + NC], T.s[:, t2:t2 + NC], T.xb[:, 0:4 * NC]).then_inc(S.q2, 1)
+    v.wait_ge(S.lw, 16)
+    v.quantize_mx(T.wq[:], T.ws[:], T.wb[:]).then_inc(S.qw, 1)
+
+    dst = cores[next(r for r in range(len(cores)) if plan[r]["from"] == rank)]
+    rid, pid = topo.addr(dst, core)
+    a, n = P["send_at"], P["send_w"]
+    m = topo.mask(core, dst)
+    ncross = 2 * len(bits(m))
+    g.wait_ge(S.q1, 1)
+    g.remote_dma(T.q[:, NC:NC + n].bitcast(dt.uint8), T.q[:, a:a + n].bitcast(dt.uint8), S.cx, S.ls, pid, rid, m)
+    g.remote_dma(T.s[:, NC:NC + n], T.s[:, a:a + n], S.cx, S.ls, pid, rid, m)
+
+    dests = P["order"][::-1]
+    common = m
+    for d in dests:
+        common &= topo.mask(core, cores[d])
+    ev, od = bits(common)[0::2], bits(common)[1::2]
+    h = len(ev) // 2
+    shares = ((ev, od[:h], od[h:]), (od, ev[:h], ev[h:]))
+    g.wait_ge(S.q2, 1)
+    g.wait_ge(S.cx, ncross)
+    for buf, share in zip((T.q, T.s), shares):
+        tr = []
+        for d, engines in zip(dests, share):
+            rid, pid = topo.addr(cores[d], core)
+            a, to = P["win"][d], plan[d]["slot"][rank]
+            src, out = buf[:, a:a + W], buf[:, to:to + W]
+            if share is shares[0]:
+                src, out = src.bitcast(dt.uint8), out.bitcast(dt.uint8)
+            tr.append(RemoteDMATransfer(dst_ids=[DstId(rid=rid, pnc=pid)], dma_engine_mask=sum(engines),
+                                        remote_sem=S["ar%d" % plan[d]["order"].index(rank)], srcs=[src], dsts=[out]))
+        g.remote_dma_fused(tr, local_sem=S.ls)
+    lands = [sum(len(share[i]) for share in shares) for i in (2, 1, 0)]
+
+    t = g.tensor
+    t.wait_ge(S.qw, 1)
+    t.wait_ge(S.q1, 1)
+    t.wait_ge(S.cx, ncross)
+    for b, (lo, hi) in enumerate(P["banks"]):
+        if b == 1:
+            t.wait_ge(S.q2, 1)
+        if b:
+            t.wait_ge(S["ar%d" % (b - 1)], lands[b - 1])
+        t.matmul_mx(T.ps[:, 512 * b:512 * b + hi - lo], T.wq[:], T.ws[:], T.q[:, lo:hi], T.s[:, lo:hi], True, True).then_inc(S["mm%d" % b], 1)
+
+    nv = ns = 0
+    for b in range(len(P["banks"])):
+        vec = b in (1, 3)
+        (v if vec else g.scalar).wait_ge(S["mm%d" % b], 1)
+        for bb, pos, c, n in P["runs"]:
+            if bb != b:
+                continue
+            out, src = T.yt[:, c:c + n], T.ps[:, 512 * b + pos:512 * b + pos + n]
+            if vec:
+                v.tensor_copy(out, src).then_inc(S.vd, 1)
+                nv += 1
+            else:
+                g.scalar.activation(out, src, ActivationFunctionType.Copy).then_inc(S.sd, 1)
+                ns += 1
+    if ns:
+        g.sync.wait_ge(S.sd, ns)
+    if nv:
+        g.sync.wait_ge(S.vd, nv)
+    g.sync.dma_start(T.y[:], T.yt[:]).then_inc(S.st, 16)
+    g.sync.wait_ge(S.st, 16)
+    g.wait_ge(S.ls, ncross + len(bits(common)) * 2)

@@ -2,9 +2,10 @@ from concourse.bass import DstId, RemoteDMATransfer
 from concourse.mybir import dt, ActivationFunctionType
 
 NC = 128
-ALIGN = 16
+BUDGET = 267520
+COLUMN = 5 * 128
 SCRATCH = {
-    "xb": ("sbuf", [128, 8 * NC], "bfloat16"),
+    "xb": ("sbuf", [128, 4 * NC], "bfloat16"),
     "wb": ("sbuf", [128, 4 * NC], "bfloat16"),
     "wq": ("sbuf", [128, NC], "float8_e4m3fn_x4"),
     "ws": ("sbuf", [128, NC], "uint8"),
@@ -13,7 +14,8 @@ SCRATCH = {
     "ps": ("psum", [128, 2048], "float32"),
     "yt": ("sbuf", [128, 2 * NC], "float32"),
 }
-SEMAPHORES = ["lx", "le", "lw", "q1", "q2", "qw", "cx", "ar0", "ar1", "ar2", "ls", "mm0", "mm1", "mm2", "mm3", "vd", "sd", "st"]
+SEMAPHORES = ["lx", "lw", "q1", "qw", "cx", "ao", "ar0", "ar1", "ar2", "ls", "mm0", "mm1", "mm2", "mm3", "vd", "sd", "st"]
+CACHE = {}
 
 
 def cyc(start, n):
@@ -26,202 +28,278 @@ def cyc(start, n):
     return out
 
 
+def bits(mask):
+    return [1 << i for i in range(mask.bit_length()) if (mask >> i) & 1]
+
+
+def matchings(left, right, ok):
+    if not left:
+        return [[]]
+    return [[(left[0], x)] + rest for x in right if ok(left[0], x)
+            for rest in matchings(left[1:], [y for y in right if y != x], ok)]
+
+
+def product(lists):
+    if not lists:
+        return [[]]
+    return [[x] + rest for x in lists[0] for rest in product(lists[1:])]
+
+
+def shortest(held, labels):
+    need, have, miss, best, lo = set(labels), {}, len(set(labels)), None, 0
+    if not need:
+        return (0, 0)
+    for hi, lab in enumerate(held):
+        if lab in need:
+            have[lab] = have.get(lab, 0) + 1
+            miss -= have[lab] == 1
+        while not miss:
+            if best is None or hi + 1 - lo < best[1]:
+                best = (lo, hi + 1 - lo)
+            if held[lo] in need:
+                have[held[lo]] -= 1
+                miss += have[held[lo]] == 0
+            lo += 1
+    return best
+
+
 def make_plan(T, topo):
     cores, cnt = T.cores, T.tables["CNT"]
     N = len(cores)
     off = [[sum(c[:e]) for e in range(N + 1)] for c in cnt]
     peers = [[j for j in range(N) if topo.host(cores[j]) == topo.host(cores[r])] for r in range(N)]
-    partner = [next(j for j in range(N) if topo.host(cores[j]) != topo.host(cores[r]) and topo.chip(cores[j]) == topo.chip(cores[r]))
-               for r in range(N)]
     blk = [[(peers[r][0] - 1 + i) % N for i in range(len(peers[r]) + 1)] for r in range(N)]
-    nb = len(blk[0])
+    np = len(peers[0])
 
-    def cross(s, L):
-        s1 = (off[s][blk[s][L]] + cnt[s][blk[s][L]]) % NC
-        c = blk[partner[s]]
-        return s1, (off[s][c[0]] - s1) % NC, sum(cnt[s][f] for f in c)
+    def labels(j, blocks):
+        return [(j, off[j][f] + i) for f in blocks for i in range(cnt[j][f])]
 
-    def windows(r, L, M, s, padl, wc):
-        own, rv = [cnt[r][f] for f in blk[r]], [cnt[s][f] for f in blk[r]]
-        res = {}
-        for k, d in enumerate(peers[r]):
-            if d == r:
+    def part(j, d):
+        k = peers[d].index(d)
+        return labels(j, blk[d][k:k + 2])
+
+    def hop1(s, r, d):
+        return labels(s, blk[r][1:] if d == peers[r][0] else blk[r][:-1] if d == peers[r][-1] else blk[r])
+
+    def tile(r, f):
+        return [(r, (off[r][f] + i) % NC) for i in range(NC)]
+
+    def one_run(row, want):
+        return shortest(row, want)[1] == len(want)
+
+    def relay(r, s, f, d):
+        row, arrived = tile(r, f), hop1(s, r, d)
+        if not one_run(row, part(r, d)):
+            return None
+        best = None
+        for side in (0, 1):
+            held = arrived + row if side else row + arrived
+            ws = {e: shortest(held, part(r, e) + part(s, e))[1] for e in peers[r] if e not in (r, d)}
+            W = max(ws.values())
+            mate = sum(W for e in ws if not topo.same_plane(cores[r], cores[e]))
+            port = sum(W for e in ws if not topo.mates(cores[r], cores[e]))
+            key = (max(3 * mate, 3 * port, 2 * W * len(ws)), sum(ws.values()), side)
+            if best is None or key < best:
+                best = key
+        return best
+
+    def ways(r, s):
+        best = {}
+        for f in range(N):
+            for h in range(N):
+                for d in peers[r]:
+                    for e in peers[s]:
+                        if d == r or e == s:
+                            continue
+                        if not all(one_run(tile(s, h), w) for w in (hop1(s, r, d), part(s, d))):
+                            continue
+                        if not all(one_run(tile(r, f), w) for w in (hop1(r, s, e), part(r, e))):
+                            continue
+                        a, b = relay(r, s, f, d), relay(s, r, h, e)
+                        if not a or not b:
+                            continue
+                        key = (max(a[0], b[0]), a[0] + b[0], a[1] + b[1], f, h)
+                        if (d, e) not in best or key < best[d, e][0]:
+                            cross = (len(hop1(s, r, d)) + len(part(s, d)), len(hop1(r, s, e)) + len(part(r, e)))
+                            best[d, e] = (key, cross, {r: (s, f, d, a[2]), s: (r, h, e, b[2])})
+        return sorted(best.values(), key=lambda x: x[0])
+
+    far = [s for s in range(N) if s not in peers[0]]
+    options = {(r, s): ways(r, s) for r in peers[0] for s in far if topo.same_plane(cores[r], cores[s])}
+    choice = None
+    for m in matchings(peers[0], far, lambda r, s: (r, s) in options):
+        for combo in product([options[p] for p in m]):
+            if max(sum(c[1][0] for c in combo), sum(c[1][1] for c in combo)) * COLUMN > BUDGET:
                 continue
-            o = []
-            if L >= k + 1:
-                a = NC - sum(own[k:L + 1])
-                o.append((NC + padl + sum(rv[:k + 2]) - a, a))
-            if M <= k:
-                a = NC + padl + sum(rv[:k])
-                o.append((NC + wc + sum(own[M:k + 2]) - a, a))
-            if not o:
-                return None
-            res[d] = min(o)
-        return res
+            key = (max(c[0][0] for c in combo), sum(c[0][1] for c in combo), sum(c[0][2] for c in combo))
+            if choice is None or key < choice[0]:
+                choice = (key, combo)
 
     plan = [None] * N
-    for r in range(N):
-        if plan[r]:
-            continue
-        p = partner[r]
-        best = None
-        for Lr in range(nb - 1):
-            for Lp in range(nb - 1):
-                two = []
-                for me, frm, Lm, Lf in ((r, p, Lr, Lp), (p, r, Lp, Lr)):
-                    s1, at, w = cross(frm, Lf)
-                    pad = -w % ALIGN
-                    cand = []
-                    for padl in range(0, pad + 1, 4):
-                        if padl > at or at + w + pad - padl > NC:
-                            continue
-                        for M in range(nb - 1):
-                            win = windows(me, Lm, M, frm, padl, w + pad)
-                            if win:
-                                ws = [v[0] for v in win.values()]
-                                cand.append((max(ws), sum(ws), -M, padl, at - padl, w + pad, win))
-                    if cand:
-                        two.append(min(cand, key=lambda c: c[:4]))
-                if len(two) == 2:
-                    key = (max(two[0][0], two[1][0]), two[0][0] + two[1][0], two[0][1] + two[1][1], Lr + Lp)
-                    if best is None or key < best[0]:
-                        best = (key, two, (Lr, Lp))
-        for me, frm, c, L in ((r, p, best[1][0], best[2][0]), (p, r, best[1][1], best[2][1])):
-            M = -c[2]
-            plan[me] = {"from": frm, "W": c[0], "recv_at": c[4], "wc": c[5], "win": {d: v[1] for d, v in c[6].items()},
-                        "s1": cross(me, L)[0], "s2": off[me][blk[me][M]], "E": sum(cnt[me][f] for f in blk[me][M:])}
+    for c in choice[1]:
+        for r, (s, f, d, side) in c[2].items():
+            plan[r] = {"from": s, "s1": off[r][f] % NC, "direct": d, "side": side}
     for r in range(N):
         P = plan[r]
-        P["send_at"] = plan[partner[r]]["recv_at"]
-        P["send_w"] = plan[partner[r]]["wc"]
-        P["tile1"] = [(r, (P["s1"] + i) % NC) for i in range(NC)]
-    for r in range(N):
-        P = plan[r]
-        arrived = plan[P["from"]]["tile1"][P["recv_at"]:P["recv_at"] + P["wc"]]
-        extra = [(r, (P["s2"] + i) % NC) for i in range(P["E"])]
-        P["cols"] = P["tile1"] + arrived + extra + P["tile1"][:NC - P["E"]]
-        P["base"] = len(P["cols"])
+        s, d = P["from"], P["direct"]
+        row, arrived = [(r, (P["s1"] + i) % NC) for i in range(NC)], hop1(s, r, d)
+        P["tile_at"], P["hop1_at"] = (NC, NC - len(arrived)) if P["side"] else (0, NC)
+        P["lo"], P["held"] = min(P["tile_at"], P["hop1_at"]), arrived + row if P["side"] else row + arrived
+        P["hi"] = P["lo"] + len(P["held"])
         P["order"] = sorted((j for j in peers[r] if j != r),
                             key=lambda j: 0 if topo.mates(cores[j], cores[r]) else 1 if topo.same_plane(cores[j], cores[r]) else 2)
+        P["ahead"], P["hop2"] = [], []
+    for r in range(N):
+        P, s = plan[r], plan[r]["from"]
+        there = plan[s]["direct"]
+        for key, e, want in (("hop1", s, hop1(r, s, there)), ("direct", there, part(r, there)), ("own", P["direct"], part(r, P["direct"]))):
+            a, w = shortest(P["held"], want)
+            if w:
+                full = bits(topo.mask(cores[r], cores[e]))
+                P["ahead"].append([(key, e, P["lo"] + a, w, full, full)])
+        win = {e: shortest(P["held"], part(r, e) + part(s, e)) for e in P["order"] if e != P["direct"]}
+        W = max(w for a, w in win.values())
+        common = -1
+        for e in win:
+            common &= topo.mask(cores[r], cores[e])
+        ev, od = bits(common)[0::2], bits(common)[1::2]
+        P["hop2"].append([("hop2", e, P["lo"] + min(a, len(P["held"]) - W), W, ec, es)
+                          for (e, (a, w)), (ec, es) in zip(win.items(), [(ev, od), (od, ev)])])
+    into = [{} for e in range(N)]
+    for r in range(N):
+        P = plan[r]
+        for call in P["ahead"] + P["hop2"]:
+            for key, e, a, w, ec, es in call:
+                into[e][key, r] = (w, P["held"][a - P["lo"]:a - P["lo"] + w], len(ec) + len(es))
     for e in range(N):
         P = plan[e]
-        P["slot"], at, lay = {}, P["base"], list(P["cols"])
-        banks = [(0, NC + P["wc"])]
-        for r in P["order"]:
-            R = plan[r]
-            P["slot"][r] = at
-            a = R["win"][e]
-            lay += R["cols"][a:a + R["W"]]
-            at += R["W"]
-            banks.append((at - max(R["W"], NC), at))
-        P["banks"] = banks
+        P["into"] = into[e]
         want = [(j, off[j][(e - k) % N] + i) for k in range(2) for j in range(N) for i in range(cnt[j][(e - k) % N])]
-        runs = []
-        for c, lab in enumerate(want):
-            b, pos = next((b, i) for b, (lo, hi) in enumerate(banks) for i in range(lo, hi) if lay[i] == lab)
-            pos -= banks[b][0]
-            if runs and runs[-1][0] == b and runs[-1][1] + runs[-1][3] == pos:
-                runs[-1][3] += 1
-            else:
-                runs.append([b, pos, c, 1])
-        P["runs"] = runs
+        early = [x for x in into[e] if x[0] in ("own", "direct")]
+        late = [("hop2", r) for r in P["order"] if ("hop2", r) in into[e]]
+        best = None
+        for alone in late[:1] if len(late) < 2 else late:
+            feeds = [[], early, [x for x in late if x != alone], [alone]]
+            P["feeds"] = feeds
+            lay, slot, banks = list(P["held"]), {("hop1", P["from"]): P["hop1_at"]}, [(P["lo"], P["hi"])]
+            for b in (1, 2, 3):
+                lo = len(lay)
+                for x in feeds[b]:
+                    slot[x] = P["lo"] + len(lay)
+                    lay += into[e][x][1]
+                banks.append((P["lo"] + min(lo, len(lay) - NC), P["lo"] + len(lay)) if len(lay) > lo else None)
+            runs = []
+            for c, lab in enumerate(want):
+                b, pos = next((b, i - bank[0]) for b, bank in enumerate(banks) if bank
+                              for i in range(bank[0], bank[1]) if lay[i - P["lo"]] == lab)
+                if runs and runs[-1][0] == b and runs[-1][1] + runs[-1][3] == pos:
+                    runs[-1][3] += 1
+                else:
+                    runs.append([b, pos, c, 1])
+            last = [sum(1 for x in runs if x[0] == b) for b in (2, 3)]
+            key = max(last[0], last[1] + 2)
+            if best is None or key < best:
+                best = key
+                P["plan"] = (slot, banks, feeds, runs)
+        if not late:
+            feeds = [[], early, [], []]
+            lay, slot = list(P["held"]), {("hop1", P["from"]): P["hop1_at"]}
+            lo = len(lay)
+            for x in early:
+                slot[x] = P["lo"] + len(lay)
+                lay += into[e][x][1]
+            banks = [(P["lo"], P["hi"]), (P["lo"] + min(lo, len(lay) - NC), P["lo"] + len(lay)), None, None]
+            runs = []
+            for c, lab in enumerate(want):
+                b, pos = next((b, i - bank[0]) for b, bank in enumerate(banks) if bank
+                              for i in range(bank[0], bank[1]) if lay[i - P["lo"]] == lab)
+                if runs and runs[-1][0] == b and runs[-1][1] + runs[-1][3] == pos:
+                    runs[-1][3] += 1
+                else:
+                    runs.append([b, pos, c, 1])
+            P["plan"] = (slot, banks, feeds, runs)
     return plan
-
-
-def bits(mask):
-    return [1 << i for i in range(mask.bit_length()) if (mask >> i) & 1]
 
 
 def rank_program(g, core, T, topo):
     rank = T.rank_of(core)
     if rank is None:
         return
-    plan = make_plan(T, topo)
+    if "plan" not in CACHE:
+        CACHE["plan"] = make_plan(T, topo)
+    plan = CACHE["plan"]
     P, S, cores = plan[rank], T.sem, T.cores
-    E, wc, W = P["E"], P["wc"], P["W"]
+    slot, banks, feeds, runs = P["plan"]
+    into = P["into"]
 
-    pieces, at = cyc(P["s1"], NC), E
+    pieces, at = cyc(P["s1"], NC), 0
     for i, (a, n) in enumerate(pieces):
         (g.sync if i == 0 else g.scalar).dma_start(T.xb[:, 4 * at:4 * (at + n)], T.x[:, 4 * a:4 * (a + n)]).then_inc(S.lx, 16)
         at += n
-    extra, at = cyc(P["s2"], E), 0
-    for a, n in extra:
-        g.sync.dma_start(T.xb[:, 4 * at:4 * (at + n)], T.x[:, 4 * a:4 * (a + n)]).then_inc(S.le, 16)
-        at += n
-    nx, ne = 16 * len(pieces), 16 * len(extra)
+    nx = 16 * len(pieces)
     g.scalar.wait_ge(S.lx, nx)
     g.scalar.dma_start(T.wb[:], T.w[:]).then_inc(S.lw, 16)
 
     v = g.vector
+    a = P["tile_at"]
     v.wait_ge(S.lx, nx)
-    v.quantize_mx(T.q[:, 0:NC], T.s[:, 0:NC], T.xb[:, 4 * E:4 * (E + NC)]).then_inc(S.q1, 1)
-    if ne:
-        v.wait_ge(S.le, ne)
-    t2 = NC + wc
-    v.quantize_mx(T.q[:, t2:t2 + NC], T.s[:, t2:t2 + NC], T.xb[:, 0:4 * NC]).then_inc(S.q2, 1)
+    v.quantize_mx(T.q[:, a:a + NC], T.s[:, a:a + NC], T.xb[:]).then_inc(S.q1, 1)
     v.wait_ge(S.lw, 16)
     v.quantize_mx(T.wq[:], T.ws[:], T.wb[:]).then_inc(S.qw, 1)
 
-    dst = cores[next(r for r in range(len(cores)) if plan[r]["from"] == rank)]
-    rid, pid = topo.addr(dst, core)
-    a, n = P["send_at"], P["send_w"]
-    m = topo.mask(core, dst)
-    ncross = 2 * len(bits(m))
+    ncross = into["hop1", P["from"]][2]
+    sent = 0
     g.wait_ge(S.q1, 1)
-    g.remote_dma(T.q[:, NC:NC + n].bitcast(dt.uint8), T.q[:, a:a + n].bitcast(dt.uint8), S.cx, S.ls, pid, rid, m)
-    g.remote_dma(T.s[:, NC:NC + n], T.s[:, a:a + n], S.cx, S.ls, pid, rid, m)
-
-    dests = P["order"][::-1]
-    common = m
-    for d in dests:
-        common &= topo.mask(core, cores[d])
-    ev, od = bits(common)[0::2], bits(common)[1::2]
-    h = len(ev) // 2
-    shares = ((ev, od[:h], od[h:]), (od, ev[:h], ev[h:]))
-    g.wait_ge(S.q2, 1)
-    g.wait_ge(S.cx, ncross)
-    for buf, share in zip((T.q, T.s), shares):
-        tr = []
-        for d, engines in zip(dests, share):
-            rid, pid = topo.addr(cores[d], core)
-            a, to = P["win"][d], plan[d]["slot"][rank]
-            src, out = buf[:, a:a + W], buf[:, to:to + W]
-            if share is shares[0]:
-                src, out = src.bitcast(dt.uint8), out.bitcast(dt.uint8)
-            tr.append(RemoteDMATransfer(dst_ids=[DstId(rid=rid, pnc=pid)], dma_engine_mask=sum(engines),
-                                        remote_sem=S["ar%d" % plan[d]["order"].index(rank)], srcs=[src], dsts=[out]))
-        g.remote_dma_fused(tr, local_sem=S.ls)
-    lands = [sum(len(share[i]) for share in shares) for i in (2, 1, 0)]
+    for calls in (P["ahead"], P["hop2"]):
+        if calls is P["hop2"]:
+            g.wait_ge(S.cx, ncross)
+        for call in calls:
+            for i, buf in enumerate((T.q, T.s)):
+                tr = []
+                for key, d, a, w, ec, es in call:
+                    rid, pid = topo.addr(cores[d], core)
+                    to, engines = plan[d]["plan"][0][key, rank], es if i else ec
+                    src, out = buf[:, a:a + w], buf[:, to:to + w]
+                    if i == 0:
+                        src, out = src.bitcast(dt.uint8), out.bitcast(dt.uint8)
+                    sem = S.cx if key == "hop1" else S["ar%d" % plan[d]["order"].index(rank)] if key == "hop2" else S.ao
+                    tr.append(RemoteDMATransfer(dst_ids=[DstId(rid=rid, pnc=pid)], dma_engine_mask=sum(engines),
+                                                remote_sem=sem, srcs=[src], dsts=[out]))
+                    sent += len(engines)
+                g.remote_dma_fused(tr, local_sem=S.ls)
 
     t = g.tensor
     t.wait_ge(S.qw, 1)
     t.wait_ge(S.q1, 1)
     t.wait_ge(S.cx, ncross)
-    for b, (lo, hi) in enumerate(P["banks"]):
+    for b, bank in enumerate(banks):
+        if not bank:
+            continue
         if b == 1:
-            t.wait_ge(S.q2, 1)
-        if b:
-            t.wait_ge(S["ar%d" % (b - 1)], lands[b - 1])
+            t.wait_ge(S.ao, sum(into[x][2] for x in feeds[1]))
+        for x in feeds[b] if b > 1 else []:
+            t.wait_ge(S["ar%d" % P["order"].index(x[1])], into[x][2])
+        lo, hi = bank
         t.matmul_mx(T.ps[:, 512 * b:512 * b + hi - lo], T.wq[:], T.ws[:], T.q[:, lo:hi], T.s[:, lo:hi], True, True).then_inc(S["mm%d" % b], 1)
 
-    nv = ns = 0
-    for b in range(len(P["banks"])):
-        vec = b in (1, 3)
+    done = {"vd": 0, "sd": 0}
+    for b, bank in enumerate(banks):
+        if not bank:
+            continue
+        vec = b in (1, 2)
         (v if vec else g.scalar).wait_ge(S["mm%d" % b], 1)
-        for bb, pos, c, n in P["runs"]:
+        for bb, pos, c, n in runs:
             if bb != b:
                 continue
             out, src = T.yt[:, c:c + n], T.ps[:, 512 * b + pos:512 * b + pos + n]
             if vec:
                 v.tensor_copy(out, src).then_inc(S.vd, 1)
-                nv += 1
             else:
                 g.scalar.activation(out, src, ActivationFunctionType.Copy).then_inc(S.sd, 1)
-                ns += 1
-    if ns:
-        g.sync.wait_ge(S.sd, ns)
-    if nv:
-        g.sync.wait_ge(S.vd, nv)
+            done["vd" if vec else "sd"] += 1
+    for k, n in done.items():
+        if n:
+            g.sync.wait_ge(S[k], n)
     g.sync.dma_start(T.y[:], T.yt[:]).then_inc(S.st, 16)
     g.sync.wait_ge(S.st, 16)
-    g.wait_ge(S.ls, ncross + len(bits(common)) * 2)
+    g.wait_ge(S.ls, sent)

from concourse.bass import DstId, RemoteDMATransfer
from concourse.mybir import dt, ActivationFunctionType

NC = 128
BUDGET = 267520
COLUMN = 5 * 128
SCRATCH = {
    "xb": ("sbuf", [128, 4 * NC], "bfloat16"),
    "wb": ("sbuf", [128, 4 * NC], "bfloat16"),
    "wq": ("sbuf", [128, NC], "float8_e4m3fn_x4"),
    "ws": ("sbuf", [128, NC], "uint8"),
    "q": ("sbuf", [128, 896], "float8_e4m3fn_x4"),
    "s": ("sbuf", [128, 896], "uint8"),
    "ps": ("psum", [128, 2048], "float32"),
    "yt": ("sbuf", [128, 2 * NC], "float32"),
}
SEMAPHORES = ["lx", "lw", "q1", "qw", "cx", "ao", "ar0", "ar1", "ar2", "ls", "mm0", "mm1", "mm2", "mm3", "vd", "sd", "st"]
CACHE = {}


def cyc(start, n):
    out = []
    start %= NC
    while n:
        m = min(n, NC - start)
        out.append((start, m))
        start, n = (start + m) % NC, n - m
    return out


def bits(mask):
    return [1 << i for i in range(mask.bit_length()) if (mask >> i) & 1]


def matchings(left, right, ok):
    if not left:
        return [[]]
    return [[(left[0], x)] + rest for x in right if ok(left[0], x)
            for rest in matchings(left[1:], [y for y in right if y != x], ok)]


def product(lists):
    if not lists:
        return [[]]
    return [[x] + rest for x in lists[0] for rest in product(lists[1:])]


def shortest(held, labels):
    need, have, miss, best, lo = set(labels), {}, len(set(labels)), None, 0
    if not need:
        return (0, 0)
    for hi, lab in enumerate(held):
        if lab in need:
            have[lab] = have.get(lab, 0) + 1
            miss -= have[lab] == 1
        while not miss:
            if best is None or hi + 1 - lo < best[1]:
                best = (lo, hi + 1 - lo)
            if held[lo] in need:
                have[held[lo]] -= 1
                miss += have[held[lo]] == 0
            lo += 1
    return best


def make_plan(T, topo):
    cores, cnt = T.cores, T.tables["CNT"]
    N = len(cores)
    off = [[sum(c[:e]) for e in range(N + 1)] for c in cnt]
    peers = [[j for j in range(N) if topo.host(cores[j]) == topo.host(cores[r])] for r in range(N)]
    blk = [[(peers[r][0] - 1 + i) % N for i in range(len(peers[r]) + 1)] for r in range(N)]
    np = len(peers[0])

    def labels(j, blocks):
        return [(j, off[j][f] + i) for f in blocks for i in range(cnt[j][f])]

    def part(j, d):
        k = peers[d].index(d)
        return labels(j, blk[d][k:k + 2])

    def hop1(s, r, d):
        return labels(s, blk[r][1:] if d == peers[r][0] else blk[r][:-1] if d == peers[r][-1] else blk[r])

    def tile(r, f):
        return [(r, (off[r][f] + i) % NC) for i in range(NC)]

    def one_run(row, want):
        return shortest(row, want)[1] == len(want)

    def relay(r, s, f, d):
        row, arrived = tile(r, f), hop1(s, r, d)
        if not one_run(row, part(r, d)):
            return None
        best = None
        for side in (0, 1):
            held = arrived + row if side else row + arrived
            ws = {e: shortest(held, part(r, e) + part(s, e))[1] for e in peers[r] if e not in (r, d)}
            W = max(ws.values())
            mate = sum(W for e in ws if not topo.same_plane(cores[r], cores[e]))
            port = sum(W for e in ws if not topo.mates(cores[r], cores[e]))
            key = (max(3 * mate, 3 * port, 2 * W * len(ws)), sum(ws.values()), side)
            if best is None or key < best:
                best = key
        return best

    def ways(r, s):
        best = {}
        for f in range(N):
            for h in range(N):
                for d in peers[r]:
                    for e in peers[s]:
                        if d == r or e == s:
                            continue
                        if not all(one_run(tile(s, h), w) for w in (hop1(s, r, d), part(s, d))):
                            continue
                        if not all(one_run(tile(r, f), w) for w in (hop1(r, s, e), part(r, e))):
                            continue
                        a, b = relay(r, s, f, d), relay(s, r, h, e)
                        if not a or not b:
                            continue
                        key = (max(a[0], b[0]), a[0] + b[0], a[1] + b[1], f, h)
                        if (d, e) not in best or key < best[d, e][0]:
                            cross = (len(hop1(s, r, d)) + len(part(s, d)), len(hop1(r, s, e)) + len(part(r, e)))
                            best[d, e] = (key, cross, {r: (s, f, d, a[2]), s: (r, h, e, b[2])})
        return sorted(best.values(), key=lambda x: x[0])

    far = [s for s in range(N) if s not in peers[0]]
    options = {(r, s): ways(r, s) for r in peers[0] for s in far if topo.same_plane(cores[r], cores[s])}
    choice = None
    for m in matchings(peers[0], far, lambda r, s: (r, s) in options):
        for combo in product([options[p] for p in m]):
            if max(sum(c[1][0] for c in combo), sum(c[1][1] for c in combo)) * COLUMN > BUDGET:
                continue
            key = (max(c[0][0] for c in combo), sum(c[0][1] for c in combo), sum(c[0][2] for c in combo))
            if choice is None or key < choice[0]:
                choice = (key, combo)

    plan = [None] * N
    for c in choice[1]:
        for r, (s, f, d, side) in c[2].items():
            plan[r] = {"from": s, "s1": off[r][f] % NC, "direct": d, "side": side}
    for r in range(N):
        P = plan[r]
        s, d = P["from"], P["direct"]
        row, arrived = [(r, (P["s1"] + i) % NC) for i in range(NC)], hop1(s, r, d)
        P["tile_at"], P["hop1_at"] = (NC, NC - len(arrived)) if P["side"] else (0, NC)
        P["lo"], P["held"] = min(P["tile_at"], P["hop1_at"]), arrived + row if P["side"] else row + arrived
        P["hi"] = P["lo"] + len(P["held"])
        P["order"] = sorted((j for j in peers[r] if j != r),
                            key=lambda j: 0 if topo.mates(cores[j], cores[r]) else 1 if topo.same_plane(cores[j], cores[r]) else 2)
        P["ahead"], P["hop2"] = [], []
    for r in range(N):
        P, s = plan[r], plan[r]["from"]
        there = plan[s]["direct"]
        for key, e, want in (("hop1", s, hop1(r, s, there)), ("direct", there, part(r, there)), ("own", P["direct"], part(r, P["direct"]))):
            a, w = shortest(P["held"], want)
            if w:
                full = bits(topo.mask(cores[r], cores[e]))
                P["ahead"].append([(key, e, P["lo"] + a, w, full, full)])
        win = {e: shortest(P["held"], part(r, e) + part(s, e)) for e in P["order"] if e != P["direct"]}
        W = max(w for a, w in win.values())
        common = -1
        for e in win:
            common &= topo.mask(cores[r], cores[e])
        ev, od = bits(common)[0::2], bits(common)[1::2]
        P["hop2"].append([("hop2", e, P["lo"] + min(a, len(P["held"]) - W), W, ec, es)
                          for (e, (a, w)), (ec, es) in zip(win.items(), [(ev, od), (od, ev)])])
    into = [{} for e in range(N)]
    for r in range(N):
        P = plan[r]
        for call in P["ahead"] + P["hop2"]:
            for key, e, a, w, ec, es in call:
                into[e][key, r] = (w, P["held"][a - P["lo"]:a - P["lo"] + w], len(ec) + len(es))
    for e in range(N):
        P = plan[e]
        P["into"] = into[e]
        want = [(j, off[j][(e - k) % N] + i) for k in range(2) for j in range(N) for i in range(cnt[j][(e - k) % N])]
        early = [x for x in into[e] if x[0] in ("own", "direct")]
        late = [("hop2", r) for r in P["order"] if ("hop2", r) in into[e]]
        best = None
        for alone in late[:1] if len(late) < 2 else late:
            feeds = [[], early, [x for x in late if x != alone], [alone]]
            P["feeds"] = feeds
            lay, slot, banks = list(P["held"]), {("hop1", P["from"]): P["hop1_at"]}, [(P["lo"], P["hi"])]
            for b in (1, 2, 3):
                lo = len(lay)
                for x in feeds[b]:
                    slot[x] = P["lo"] + len(lay)
                    lay += into[e][x][1]
                banks.append((P["lo"] + min(lo, len(lay) - NC), P["lo"] + len(lay)) if len(lay) > lo else None)
            runs = []
            for c, lab in enumerate(want):
                b, pos = next((b, i - bank[0]) for b, bank in enumerate(banks) if bank
                              for i in range(bank[0], bank[1]) if lay[i - P["lo"]] == lab)
                if runs and runs[-1][0] == b and runs[-1][1] + runs[-1][3] == pos:
                    runs[-1][3] += 1
                else:
                    runs.append([b, pos, c, 1])
            last = [sum(1 for x in runs if x[0] == b) for b in (2, 3)]
            key = max(last[0], last[1] + 2)
            if best is None or key < best:
                best = key
                P["plan"] = (slot, banks, feeds, runs)
        if not late:
            feeds = [[], early, [], []]
            lay, slot = list(P["held"]), {("hop1", P["from"]): P["hop1_at"]}
            lo = len(lay)
            for x in early:
                slot[x] = P["lo"] + len(lay)
                lay += into[e][x][1]
            banks = [(P["lo"], P["hi"]), (P["lo"] + min(lo, len(lay) - NC), P["lo"] + len(lay)), None, None]
            runs = []
            for c, lab in enumerate(want):
                b, pos = next((b, i - bank[0]) for b, bank in enumerate(banks) if bank
                              for i in range(bank[0], bank[1]) if lay[i - P["lo"]] == lab)
                if runs and runs[-1][0] == b and runs[-1][1] + runs[-1][3] == pos:
                    runs[-1][3] += 1
                else:
                    runs.append([b, pos, c, 1])
            P["plan"] = (slot, banks, feeds, runs)
    return plan


def rank_program(g, core, T, topo):
    rank = T.rank_of(core)
    if rank is None:
        return
    if "plan" not in CACHE:
        CACHE["plan"] = make_plan(T, topo)
    plan = CACHE["plan"]
    P, S, cores = plan[rank], T.sem, T.cores
    slot, banks, feeds, runs = P["plan"]
    into = P["into"]

    pieces, at = cyc(P["s1"], NC), 0
    for i, (a, n) in enumerate(pieces):
        (g.sync if i == 0 else g.scalar).dma_start(T.xb[:, 4 * at:4 * (at + n)], T.x[:, 4 * a:4 * (a + n)]).then_inc(S.lx, 16)
        at += n
    nx = 16 * len(pieces)
    g.scalar.wait_ge(S.lx, nx)
    g.scalar.dma_start(T.wb[:], T.w[:]).then_inc(S.lw, 16)

    v = g.vector
    a = P["tile_at"]
    v.wait_ge(S.lx, nx)
    v.quantize_mx(T.q[:, a:a + NC], T.s[:, a:a + NC], T.xb[:]).then_inc(S.q1, 1)
    v.wait_ge(S.lw, 16)
    v.quantize_mx(T.wq[:], T.ws[:], T.wb[:]).then_inc(S.qw, 1)

    ncross = into["hop1", P["from"]][2]
    sent = 0
    g.wait_ge(S.q1, 1)
    for calls in (P["ahead"], P["hop2"]):
        if calls is P["hop2"]:
            g.wait_ge(S.cx, ncross)
        for call in calls:
            for i, buf in enumerate((T.q, T.s)):
                tr = []
                for key, d, a, w, ec, es in call:
                    rid, pid = topo.addr(cores[d], core)
                    to, engines = plan[d]["plan"][0][key, rank], es if i else ec
                    src, out = buf[:, a:a + w], buf[:, to:to + w]
                    if i == 0:
                        src, out = src.bitcast(dt.uint8), out.bitcast(dt.uint8)
                    sem = S.cx if key == "hop1" else S["ar%d" % plan[d]["order"].index(rank)] if key == "hop2" else S.ao
                    tr.append(RemoteDMATransfer(dst_ids=[DstId(rid=rid, pnc=pid)], dma_engine_mask=sum(engines),
                                                remote_sem=sem, srcs=[src], dsts=[out]))
                    sent += len(engines)
                g.remote_dma_fused(tr, local_sem=S.ls)

    t = g.tensor
    t.wait_ge(S.qw, 1)
    t.wait_ge(S.q1, 1)
    t.wait_ge(S.cx, ncross)
    for b, bank in enumerate(banks):
        if not bank:
            continue
        if b == 1:
            t.wait_ge(S.ao, sum(into[x][2] for x in feeds[1]))
        for x in feeds[b] if b > 1 else []:
            t.wait_ge(S["ar%d" % P["order"].index(x[1])], into[x][2])
        lo, hi = bank
        t.matmul_mx(T.ps[:, 512 * b:512 * b + hi - lo], T.wq[:], T.ws[:], T.q[:, lo:hi], T.s[:, lo:hi], True, True).then_inc(S["mm%d" % b], 1)

    done = {"vd": 0, "sd": 0}
    for b, bank in enumerate(banks):
        if not bank:
            continue
        vec = b in (1, 2)
        (v if vec else g.scalar).wait_ge(S["mm%d" % b], 1)
        for bb, pos, c, n in runs:
            if bb != b:
                continue
            out, src = T.yt[:, c:c + n], T.ps[:, 512 * b + pos:512 * b + pos + n]
            if vec:
                v.tensor_copy(out, src).then_inc(S.vd, 1)
            else:
                g.scalar.activation(out, src, ActivationFunctionType.Copy).then_inc(S.sd, 1)
            done["vd" if vec else "sd"] += 1
    for k, n in done.items():
        if n:
            g.sync.wait_ge(S[k], n)
    g.sync.dma_start(T.y[:], T.yt[:]).then_inc(S.st, 16)
    g.sync.wait_ge(S.st, 16)
    g.wait_ge(S.ls, sent)
